import numpy as np
import ml_dtypes

BF16 = ml_dtypes.bfloat16


def bf(x):
    return np.asarray(x, np.float32).astype(BF16)


def f32(x):
    return np.asarray(x, np.float32)


def f64(x):
    return np.asarray(x).astype(np.float64)


def striped(idx):
    return np.concatenate([l.reshape(-1, 16).T for l in idx])


def rows(idx, k):
    return np.tile(np.repeat(idx, 16, axis=0), (k // (16 * 8), 1))


def look(tab, idx):
    return np.take_along_axis(f64(tab), rows(idx, len(tab)), axis=1)


K, S, V, N, M = 256, 2048, 1536, 1536, 256


def setup_inputs():
    return {"tab": f32(np.random.standard_normal((2, K, S))), "y": f32(np.random.standard_normal((K, V))), "w": bf(np.random.standard_normal((K, M)) / np.sqrt(K)), "b": f32(0.5 * np.random.standard_normal((M, 1))), "offs": striped(np.stack([np.random.permutation(S)[:N] for _ in range(8)]))}


def reference(tab, y, w, b, offs):
    idx = np.stack([g.T.reshape(-1) for g in np.split(offs, 8)])
    x = (look(tab[0], idx) + f64(y)) * (np.tanh(look(tab[1], idx)))
    return np.maximum(f64(w).T @ x + f64(b), 0.0)

@@ -1,0 +1,70 @@
+from contextlib import ExitStack
+
+import concourse.mybir as mybir
+
+F32, BF16, U16 = mybir.dt.float32, mybir.dt.bfloat16, mybir.dt.uint16
+ADD, MULT, MAX = mybir.AluOpType.add, mybir.AluOpType.mult, mybir.AluOpType.max
+TANH = mybir.ActivationFunctionType.Tanh
+
+P = 128
+ROWS, PLACES = 256, 2048
+N, M = 1536, 256
+BLOCKS, HALVES = ROWS // P, M // P
+PIECE = 512
+PIECES = N // PIECE
+LIST_COLUMNS = PIECE // 16
+
+FLOPS = 2 * ROWS * M * N
+
+
+def tile_lookup_vg_addtanh_relu_kernel(tc, tab, y, w, b, offs, out):
+    nc = tc.nc
+    with ExitStack() as stack:
+        held = stack.enter_context(tc.tile_pool(name="held", bufs=1))
+        psum = stack.enter_context(tc.psum_pool(name="psum", bufs=1))
+
+        lists = held.tile([P, N // 16], U16, name="lists")
+        nc.sync.dma_start(lists[:], offs)
+
+        values, gates, streams = [], [], []
+        for k in range(BLOCKS):
+            rows = slice(k * P, (k + 1) * P)
+            values.append(held.tile([P, PLACES], F32, name=f"values{k}"))
+            nc.sync.dma_start(values[k][:], tab[0, rows, :])
+            streams.append(held.tile([P, N], F32, name=f"streams{k}"))
+            nc.sync.dma_start(streams[k][:], y[rows, :])
+            gates.append(held.tile([P, PLACES], F32, name=f"gates{k}"))
+            nc.sync.dma_start(gates[k][:], tab[1, rows, :])
+
+        weights = []
+        for k in range(BLOCKS):
+            weights.append(held.tile([P, M], BF16, name=f"weights{k}"))
+            nc.gpsimd.dma_start(weights[k][:], w[k * P : (k + 1) * P, :])
+        bias = []
+        for h in range(HALVES):
+            bias.append(held.tile([P, 1], F32, name=f"bias{h}"))
+            nc.gpsimd.dma_start(bias[h][:], b[h * P : (h + 1) * P, :])
+
+        sums = [[psum.tile([P, PIECE], F32, name=f"sums{i}_{h}") for h in range(HALVES)] for i in range(PIECES)]
+
+        for k in range(BLOCKS):
+            for i in range(PIECES):
+                columns = slice(i * PIECE, (i + 1) * PIECE)
+                entries = lists[:, i * LIST_COLUMNS : (i + 1) * LIST_COLUMNS]
+                summed = held.tile([P, PIECE], F32, name=f"summed{k}_{i}")
+                nc.vector.tensor_tensor(summed[:], values[k][:].indirect(entries), streams[k][:, columns], ADD)
+                opened = held.tile([P, PIECE], F32, name=f"opened{k}_{i}")
+                nc.scalar.activation(opened[:], gates[k][:].indirect(entries), TANH)
+                x = held.tile([P, PIECE], BF16, name=f"x{k}_{i}")
+                nc.vector.tensor_tensor(x[:], summed[:], opened[:], MULT)
+                for h in range(HALVES):
+                    nc.tensor.matmul(
+                        sums[i][h][:], weights[k][:, h * P : (h + 1) * P], x[:],
+                        start=(k == 0), stop=(k == BLOCKS - 1),
+                    )
+
+        for i in range(PIECES):
+            for h in range(HALVES):
+                result = held.tile([P, PIECE], F32, name=f"result{i}_{h}")
+                nc.vector.tensor_scalar(result[:], sums[i][h][:], bias[h][:], 0.0, op0=ADD, op1=MAX)
+                nc.sync.dma_start(out[h * P : (h + 1) * P, i * PIECE : (i + 1) * PIECE], result[:])

@@ -4,7 +4,7 @@ import concourse.mybir as mybir
 
 F32, BF16, U16 = mybir.dt.float32, mybir.dt.bfloat16, mybir.dt.uint16
 ADD, MULT, MAX = mybir.AluOpType.add, mybir.AluOpType.mult, mybir.AluOpType.max
-TANH = mybir.ActivationFunctionType.Tanh
+TANH, RELU = mybir.ActivationFunctionType.Tanh, mybir.ActivationFunctionType.Relu
 
 P = 128
 ROWS, PLACES = 256, 2048
@@ -26,45 +26,53 @@ def tile_lookup_vg_addtanh_relu_kernel(tc, tab, y, w, b, offs, out):
         lists = held.tile([P, N // 16], U16, name="lists")
         nc.sync.dma_start(lists[:], offs)
 
-        values, gates, streams = [], [], []
-        for k in range(BLOCKS):
-            rows = slice(k * P, (k + 1) * P)
-            values.append(held.tile([P, PLACES], F32, name=f"values{k}"))
-            nc.sync.dma_start(values[k][:], tab[0, rows, :])
-            streams.append(held.tile([P, N], F32, name=f"streams{k}"))
-            nc.sync.dma_start(streams[k][:], y[rows, :])
-            gates.append(held.tile([P, PLACES], F32, name=f"gates{k}"))
-            nc.sync.dma_start(gates[k][:], tab[1, rows, :])
+        zero = held.tile([P, 1], F32, name="zero")
+        nc.vector.memset(zero[:], 0.0)
+        warmed = held.tile([P, 1], F32, name="warmed")
+        nc.scalar.activation(warmed[:], zero[:], TANH)
 
-        weights = []
-        for k in range(BLOCKS):
-            weights.append(held.tile([P, M], BF16, name=f"weights{k}"))
-            nc.gpsimd.dma_start(weights[k][:], w[k * P : (k + 1) * P, :])
-        bias = []
-        for h in range(HALVES):
-            bias.append(held.tile([P, 1], F32, name=f"bias{h}"))
-            nc.gpsimd.dma_start(bias[h][:], b[h * P : (h + 1) * P, :])
+        values = [held.tile([P, PLACES], F32, name=f"values{k}") for k in range(BLOCKS)]
+        gates = [held.tile([P, PLACES], F32, name=f"gates{k}") for k in range(BLOCKS)]
+        streams = [held.tile([P, N], F32, name=f"streams{k}") for k in range(BLOCKS)]
+        weights = held.tile([P, BLOCKS, M], BF16, name="weights")
+        bias = held.tile([P, HALVES, 1], F32, name="bias")
+        first, last = slice(0, P), slice(P, ROWS)
+        nc.sync.dma_start(values[0][:], tab[0, first, :])
+        nc.sync.dma_start(streams[0][:], y[first, :])
+        nc.sync.dma_start(gates[0][:], tab[1, first, :])
+        nc.sync.dma_start(weights[:], w.rearrange("(k p) m -> p k m", p=P))
+        nc.sync.dma_start(values[1][:], tab[0, last, :])
+        nc.sync.dma_start(streams[1][:, :PIECE], y[last, :PIECE])
+        nc.sync.dma_start(gates[1][:], tab[1, last, :])
+        for i in range(1, PIECES):
+            columns = slice(i * PIECE, (i + 1) * PIECE)
+            nc.sync.dma_start(streams[1][:, columns], y[last, columns])
+        nc.sync.dma_start(bias[:], b.rearrange("(h p) o -> p h o", p=P))
 
         sums = [[psum.tile([P, PIECE], F32, name=f"sums{i}_{h}") for h in range(HALVES)] for i in range(PIECES)]
 
         for k in range(BLOCKS):
+            summed = [held.tile([P, PIECE], F32, name=f"summed{k}_{i}") for i in range(PIECES)]
+            opened = [held.tile([P, PIECE], F32, name=f"opened{k}_{i}") for i in range(PIECES)]
             for i in range(PIECES):
                 columns = slice(i * PIECE, (i + 1) * PIECE)
                 entries = lists[:, i * LIST_COLUMNS : (i + 1) * LIST_COLUMNS]
-                summed = held.tile([P, PIECE], F32, name=f"summed{k}_{i}")
-                nc.vector.tensor_tensor(summed[:], values[k][:].indirect(entries), streams[k][:, columns], ADD)
-                opened = held.tile([P, PIECE], F32, name=f"opened{k}_{i}")
-                nc.scalar.activation(opened[:], gates[k][:].indirect(entries), TANH)
+                nc.vector.tensor_tensor(summed[i][:], values[k][:].indirect(entries), streams[k][:, columns], ADD)
+                nc.scalar.activation(opened[i][:], gates[k][:].indirect(entries), TANH)
+            for i in range(PIECES):
                 x = held.tile([P, PIECE], BF16, name=f"x{k}_{i}")
-                nc.vector.tensor_tensor(x[:], summed[:], opened[:], MULT)
+                nc.vector.tensor_tensor(x[:], summed[i][:], opened[i][:], MULT)
                 for h in range(HALVES):
                     nc.tensor.matmul(
-                        sums[i][h][:], weights[k][:, h * P : (h + 1) * P], x[:],
+                        sums[i][h][:], weights[:, k, h * P : (h + 1) * P], x[:],
                         start=(k == 0), stop=(k == BLOCKS - 1),
                     )
 
         for i in range(PIECES):
             for h in range(HALVES):
                 result = held.tile([P, PIECE], F32, name=f"result{i}_{h}")
-                nc.vector.tensor_scalar(result[:], sums[i][h][:], bias[h][:], 0.0, op0=ADD, op1=MAX)
+                if i < PIECES - 1:
+                    nc.scalar.activation(result[:], sums[i][h][:], RELU, bias=bias[:, h, :])
+                else:
+                    nc.vector.tensor_scalar(result[:], sums[i][h][:], bias[:, h, :], 0.0, op0=ADD, op1=MAX)
                 nc.sync.dma_start(out[h * P : (h + 1) * P, i * PIECE : (i + 1) * PIECE], result[:])

from contextlib import ExitStack

import concourse.mybir as mybir

F32, BF16, U16 = mybir.dt.float32, mybir.dt.bfloat16, mybir.dt.uint16
ADD, MULT, MAX = mybir.AluOpType.add, mybir.AluOpType.mult, mybir.AluOpType.max
TANH, RELU = mybir.ActivationFunctionType.Tanh, mybir.ActivationFunctionType.Relu

P = 128
ROWS, PLACES = 256, 2048
N, M = 1536, 256
BLOCKS, HALVES = ROWS // P, M // P
PIECE = 512
PIECES = N // PIECE
LIST_COLUMNS = PIECE // 16

FLOPS = 2 * ROWS * M * N


def tile_lookup_vg_addtanh_relu_kernel(tc, tab, y, w, b, offs, out):
    nc = tc.nc
    with ExitStack() as stack:
        held = stack.enter_context(tc.tile_pool(name="held", bufs=1))
        psum = stack.enter_context(tc.psum_pool(name="psum", bufs=1))

        lists = held.tile([P, N // 16], U16, name="lists")
        nc.sync.dma_start(lists[:], offs)

        zero = held.tile([P, 1], F32, name="zero")
        nc.vector.memset(zero[:], 0.0)
        warmed = held.tile([P, 1], F32, name="warmed")
        nc.scalar.activation(warmed[:], zero[:], TANH)

        values = [held.tile([P, PLACES], F32, name=f"values{k}") for k in range(BLOCKS)]
        gates = [held.tile([P, PLACES], F32, name=f"gates{k}") for k in range(BLOCKS)]
        streams = [held.tile([P, N], F32, name=f"streams{k}") for k in range(BLOCKS)]
        weights = held.tile([P, BLOCKS, M], BF16, name="weights")
        bias = held.tile([P, HALVES, 1], F32, name="bias")
        first, last = slice(0, P), slice(P, ROWS)
        nc.sync.dma_start(values[0][:], tab[0, first, :])
        nc.sync.dma_start(streams[0][:], y[first, :])
        nc.sync.dma_start(gates[0][:], tab[1, first, :])
        nc.sync.dma_start(weights[:], w.rearrange("(k p) m -> p k m", p=P))
        nc.sync.dma_start(values[1][:], tab[0, last, :])
        nc.sync.dma_start(streams[1][:, :PIECE], y[last, :PIECE])
        nc.sync.dma_start(gates[1][:], tab[1, last, :])
        for i in range(1, PIECES):
            columns = slice(i * PIECE, (i + 1) * PIECE)
            nc.sync.dma_start(streams[1][:, columns], y[last, columns])
        nc.sync.dma_start(bias[:], b.rearrange("(h p) o -> p h o", p=P))

        sums = [[psum.tile([P, PIECE], F32, name=f"sums{i}_{h}") for h in range(HALVES)] for i in range(PIECES)]

        for k in range(BLOCKS):
            summed = [held.tile([P, PIECE], F32, name=f"summed{k}_{i}") for i in range(PIECES)]
            opened = [held.tile([P, PIECE], F32, name=f"opened{k}_{i}") for i in range(PIECES)]
            for i in range(PIECES):
                columns = slice(i * PIECE, (i + 1) * PIECE)
                entries = lists[:, i * LIST_COLUMNS : (i + 1) * LIST_COLUMNS]
                nc.vector.tensor_tensor(summed[i][:], values[k][:].indirect(entries), streams[k][:, columns], ADD)
                nc.scalar.activation(opened[i][:], gates[k][:].indirect(entries), TANH)
            for i in range(PIECES):
                x = held.tile([P, PIECE], BF16, name=f"x{k}_{i}")
                nc.vector.tensor_tensor(x[:], summed[i][:], opened[i][:], MULT)
                for h in range(HALVES):
                    nc.tensor.matmul(
                        sums[i][h][:], weights[:, k, h * P : (h + 1) * P], x[:],
                        start=(k == 0), stop=(k == BLOCKS - 1),
                    )

        for i in range(PIECES):
            for h in range(HALVES):
                result = held.tile([P, PIECE], F32, name=f"result{i}_{h}")
                if i < PIECES - 1:
                    nc.scalar.activation(result[:], sums[i][h][:], RELU, bias=bias[:, h, :])
                else:
                    nc.vector.tensor_scalar(result[:], sums[i][h][:], bias[:, h, :], 0.0, op0=ADD, op1=MAX)
                nc.sync.dma_start(out[h * P : (h + 1) * P, i * PIECE : (i + 1) * PIECE], result[:])
